import numpy as np
import ml_dtypes

BF16 = ml_dtypes.bfloat16


def bf(x):
    return np.asarray(x, np.float32).astype(BF16)


def f32(x):
    return np.asarray(x, np.float32)


def f64(x):
    return np.asarray(x).astype(np.float64)


def striped(idx):
    return np.tile(idx.reshape(-1, 16).T, (8, 1))


S, K, M, N = 512, 256, 256, 256


def setup_inputs():
    return {"base": bf(np.random.standard_normal((M, S))), "x": bf(np.random.standard_normal((K, N))), "w": bf(np.random.standard_normal((K, M)) / np.sqrt(K)), "c": f32(0.2 + 0.8 * np.random.random_sample((1, S))), "offs": striped(np.random.permutation(S)[:N])}


def reference(base, x, w, c, offs):
    idx = offs[:16].T.reshape(-1)
    z = f64(base).copy()
    z[:, idx] += f64(w).T @ f64(x)
    return z * f64(c)

@@ -1,0 +1,53 @@
+import concourse.mybir as mybir
+from concourse.masks import make_identity
+
+P = 128
+S, K, M, N = 512, 256, 256, 256
+K_BLOCKS = K // P
+M_BLOCKS = M // P
+FLOPS = 2 * K * M * N
+
+BF16, F32, U16 = mybir.dt.bfloat16, mybir.dt.float32, mybir.dt.uint16
+
+
+def tile_scatter_matmul_kernel(tc, base, x, w, c, offs, out):
+    nc = tc.nc
+    with (
+        tc.tile_pool(name="held", bufs=1) as held,
+        tc.psum_pool(name="banks", bufs=1) as banks,
+    ):
+        offsets = held.tile([P, N // 16], U16, name="offsets")
+        nc.sync.dma_start(offsets[:], offs)
+
+        base_sb = held.tile([P, M_BLOCKS, S], BF16, name="base_sb")
+        nc.sync.dma_start(base_sb[:], base.rearrange("(a p) s -> p a s", p=P))
+        w_sb = held.tile([P, K_BLOCKS, M], BF16, name="w_sb")
+        nc.scalar.dma_start(w_sb[:], w.rearrange("(a p) m -> p a m", p=P))
+        x_sb = held.tile([P, K_BLOCKS, N], BF16, name="x_sb")
+        nc.scalar.dma_start(x_sb[:], x.rearrange("(a p) n -> p a n", p=P))
+
+        c_sb = held.tile([P, S], F32, name="c_sb")
+        nc.gpsimd.dma_start(c_sb[:], c.partition_broadcast(P))
+
+        ident = held.tile([P, P], BF16, name="ident")
+        make_identity(nc, ident[:])
+
+        windows = [banks.tile([P, S], F32, name=f"window{mb}") for mb in range(M_BLOCKS)]
+        for mb in range(M_BLOCKS):
+            nc.tensor.matmul(windows[mb][:], ident[:], base_sb[:, mb, :], start=True, stop=False)
+
+        for mb in range(M_BLOCKS):
+            for kb in range(K_BLOCKS):
+                nc.tensor.matmul(
+                    windows[mb][:].indirect(offsets[:]),
+                    w_sb[:, kb, mb * P : (mb + 1) * P],
+                    x_sb[:, kb, :],
+                    start=False,
+                    stop=(kb == K_BLOCKS - 1),
+                )
+
+        for mb in range(M_BLOCKS):
+            scaled = held.tile([P, S], F32, name=f"scaled{mb}")
+            nc.vector.tensor_tensor(scaled[:], windows[mb][:], c_sb[:], mybir.AluOpType.mult)
+            store_queue = nc.sync if mb % 2 == 0 else nc.scalar
+            store_queue.dma_start(out[mb * P : (mb + 1) * P, :], scaled[:])

@@ -19,22 +19,23 @@ def tile_scatter_matmul_kernel(tc, base, x, w, c, offs, out):
         offsets = held.tile([P, N // 16], U16, name="offsets")
         nc.sync.dma_start(offsets[:], offs)
 
-        base_sb = held.tile([P, M_BLOCKS, S], BF16, name="base_sb")
-        nc.sync.dma_start(base_sb[:], base.rearrange("(a p) s -> p a s", p=P))
+        ident = held.tile([P, P], BF16, name="ident")
+        make_identity(nc, ident[:])
+
+        base_sb = [held.tile([P, S], BF16, name=f"base_sb{mb}") for mb in range(M_BLOCKS)]
+        nc.sync.dma_start(base_sb[0][:], base[0:P, :])
+        nc.scalar.dma_start(base_sb[1][:], base[P : 2 * P, :])
         w_sb = held.tile([P, K_BLOCKS, M], BF16, name="w_sb")
-        nc.scalar.dma_start(w_sb[:], w.rearrange("(a p) m -> p a m", p=P))
+        nc.sync.dma_start(w_sb[:], w.rearrange("(a p) m -> p a m", p=P))
         x_sb = held.tile([P, K_BLOCKS, N], BF16, name="x_sb")
         nc.scalar.dma_start(x_sb[:], x.rearrange("(a p) n -> p a n", p=P))
 
         c_sb = held.tile([P, S], F32, name="c_sb")
-        nc.gpsimd.dma_start(c_sb[:], c.partition_broadcast(P))
-
-        ident = held.tile([P, P], BF16, name="ident")
-        make_identity(nc, ident[:])
+        nc.scalar.dma_start(c_sb[:], c.partition_broadcast(P))
 
         windows = [banks.tile([P, S], F32, name=f"window{mb}") for mb in range(M_BLOCKS)]
         for mb in range(M_BLOCKS):
-            nc.tensor.matmul(windows[mb][:], ident[:], base_sb[:, mb, :], start=True, stop=False)
+            nc.tensor.matmul(windows[mb][:], ident[:], base_sb[mb][:], start=True, stop=False)
 
         for mb in range(M_BLOCKS):
             for kb in range(K_BLOCKS):

@@ -24,14 +24,20 @@ def tile_scatter_matmul_kernel(tc, base, x, w, c, offs, out):
 
         base_sb = [held.tile([P, S], BF16, name=f"base_sb{mb}") for mb in range(M_BLOCKS)]
         nc.sync.dma_start(base_sb[0][:], base[0:P, :])
+        c_row = held.tile([1, S], F32, name="c_row")
+        nc.scalar.dma_start(c_row[:], c)
         nc.scalar.dma_start(base_sb[1][:], base[P : 2 * P, :])
         w_sb = held.tile([P, K_BLOCKS, M], BF16, name="w_sb")
         nc.sync.dma_start(w_sb[:], w.rearrange("(a p) m -> p a m", p=P))
         x_sb = held.tile([P, K_BLOCKS, N], BF16, name="x_sb")
         nc.scalar.dma_start(x_sb[:], x.rearrange("(a p) n -> p a n", p=P))
 
+        ones_row = held.tile([1, P], F32, name="ones_row")
+        nc.vector.memset(ones_row[:], 1.0)
+        c_bank = banks.tile([P, S], F32, name="c_bank")
+        nc.tensor.matmul(c_bank[:], ones_row[:], c_row[:], start=True, stop=True)
         c_sb = held.tile([P, S], F32, name="c_sb")
-        nc.scalar.dma_start(c_sb[:], c.partition_broadcast(P))
+        nc.vector.tensor_copy(c_sb[:], c_bank[:])
 
         windows = [banks.tile([P, S], F32, name=f"window{mb}") for mb in range(M_BLOCKS)]
         for mb in range(M_BLOCKS):

@@ -5,6 +5,7 @@ P = 128
 S, K, M, N = 512, 256, 256, 256
 K_BLOCKS = K // P
 M_BLOCKS = M // P
+C_PLACES = S // P
 FLOPS = 2 * K * M * N
 
 BF16, F32, U16 = mybir.dt.bfloat16, mybir.dt.float32, mybir.dt.uint16
@@ -24,24 +25,27 @@ def tile_scatter_matmul_kernel(tc, base, x, w, c, offs, out):
 
         base_sb = [held.tile([P, S], BF16, name=f"base_sb{mb}") for mb in range(M_BLOCKS)]
         nc.sync.dma_start(base_sb[0][:], base[0:P, :])
-        c_row = held.tile([1, S], F32, name="c_row")
-        nc.scalar.dma_start(c_row[:], c)
         nc.scalar.dma_start(base_sb[1][:], base[P : 2 * P, :])
+        c_col = held.tile([P, C_PLACES], F32, name="c_col")
+        nc.scalar.dma_start(c_col[:], c.rearrange("o (p r) -> p (o r)", r=C_PLACES))
         w_sb = held.tile([P, K_BLOCKS, M], BF16, name="w_sb")
         nc.sync.dma_start(w_sb[:], w.rearrange("(a p) m -> p a m", p=P))
         x_sb = held.tile([P, K_BLOCKS, N], BF16, name="x_sb")
         nc.scalar.dma_start(x_sb[:], x.rearrange("(a p) n -> p a n", p=P))
 
-        ones_row = held.tile([1, P], F32, name="ones_row")
-        nc.vector.memset(ones_row[:], 1.0)
-        c_bank = banks.tile([P, S], F32, name="c_bank")
-        nc.tensor.matmul(c_bank[:], ones_row[:], c_row[:], start=True, stop=True)
-        c_sb = held.tile([P, S], F32, name="c_sb")
-        nc.vector.tensor_copy(c_sb[:], c_bank[:])
-
         windows = [banks.tile([P, S], F32, name=f"window{mb}") for mb in range(M_BLOCKS)]
         for mb in range(M_BLOCKS):
             nc.tensor.matmul(windows[mb][:], ident[:], base_sb[mb][:], start=True, stop=False)
+
+        ident_f32 = held.tile([P, P], F32, name="ident_f32")
+        nc.vector.tensor_copy(ident_f32[:], ident[:])
+        c_bank = banks.tile([P, C_PLACES, P], F32, name="c_bank")
+        for r in range(C_PLACES):
+            nc.tensor.transpose(c_bank[:, r, :], c_col[:, r : r + 1].to_broadcast([P, P]), ident_f32[:])
+        c_sb = held.tile([P, S], F32, name="c_sb")
+        nc.vector.tensor_copy(
+            c_sb[:].rearrange("p (k r) -> p k r", r=C_PLACES), c_bank[:].rearrange("p r k -> p k r")
+        )
 
         for mb in range(M_BLOCKS):
             for kb in range(K_BLOCKS):

@@ -6,6 +6,7 @@ S, K, M, N = 512, 256, 256, 256
 K_BLOCKS = K // P
 M_BLOCKS = M // P
 C_PLACES = S // P
+WARM_UPS = 8
 FLOPS = 2 * K * M * N
 
 BF16, F32, U16 = mybir.dt.bfloat16, mybir.dt.float32, mybir.dt.uint16
@@ -22,6 +23,10 @@ def tile_scatter_matmul_kernel(tc, base, x, w, c, offs, out):
 
         ident = held.tile([P, P], BF16, name="ident")
         make_identity(nc, ident[:])
+
+        warm_bank = banks.tile([P, P], F32, name="warm_bank")
+        for i in range(WARM_UPS):
+            nc.tensor.matmul(warm_bank[:], ident[:], ident[:], start=True, stop=True)
 
         base_sb = [held.tile([P, S], BF16, name=f"base_sb{mb}") for mb in range(M_BLOCKS)]
         nc.sync.dma_start(base_sb[0][:], base[0:P, :])

@@ -28,19 +28,15 @@ def tile_scatter_matmul_kernel(tc, base, x, w, c, offs, out):
         for i in range(WARM_UPS):
             nc.tensor.matmul(warm_bank[:], ident[:], ident[:], start=True, stop=True)
 
+        c_col = held.tile([P, C_PLACES], F32, name="c_col")
+        nc.scalar.dma_start(c_col[:], c.rearrange("o (p r) -> p (o r)", r=C_PLACES))
         base_sb = [held.tile([P, S], BF16, name=f"base_sb{mb}") for mb in range(M_BLOCKS)]
         nc.sync.dma_start(base_sb[0][:], base[0:P, :])
         nc.scalar.dma_start(base_sb[1][:], base[P : 2 * P, :])
-        c_col = held.tile([P, C_PLACES], F32, name="c_col")
-        nc.scalar.dma_start(c_col[:], c.rearrange("o (p r) -> p (o r)", r=C_PLACES))
         w_sb = held.tile([P, K_BLOCKS, M], BF16, name="w_sb")
         nc.sync.dma_start(w_sb[:], w.rearrange("(a p) m -> p a m", p=P))
         x_sb = held.tile([P, K_BLOCKS, N], BF16, name="x_sb")
         nc.scalar.dma_start(x_sb[:], x.rearrange("(a p) n -> p a n", p=P))
-
-        windows = [banks.tile([P, S], F32, name=f"window{mb}") for mb in range(M_BLOCKS)]
-        for mb in range(M_BLOCKS):
-            nc.tensor.matmul(windows[mb][:], ident[:], base_sb[mb][:], start=True, stop=False)
 
         ident_f32 = held.tile([P, P], F32, name="ident_f32")
         nc.vector.tensor_copy(ident_f32[:], ident[:])
@@ -51,6 +47,10 @@ def tile_scatter_matmul_kernel(tc, base, x, w, c, offs, out):
         nc.vector.tensor_copy(
             c_sb[:].rearrange("p (k r) -> p k r", r=C_PLACES), c_bank[:].rearrange("p r k -> p k r")
         )
+
+        windows = [banks.tile([P, S], F32, name=f"window{mb}") for mb in range(M_BLOCKS)]
+        for mb in range(M_BLOCKS):
+            nc.tensor.matmul(windows[mb][:], ident[:], base_sb[mb][:], start=True, stop=False)
 
         for mb in range(M_BLOCKS):
             for kb in range(K_BLOCKS):

@@ -34,9 +34,9 @@ def tile_scatter_matmul_kernel(tc, base, x, w, c, offs, out):
         nc.sync.dma_start(base_sb[0][:], base[0:P, :])
         nc.scalar.dma_start(base_sb[1][:], base[P : 2 * P, :])
         w_sb = held.tile([P, K_BLOCKS, M], BF16, name="w_sb")
-        nc.sync.dma_start(w_sb[:], w.rearrange("(a p) m -> p a m", p=P))
+        nc.sync.dma_start(w_sb[:], w.rearrange("(p a) m -> p a m", a=K_BLOCKS))
         x_sb = held.tile([P, K_BLOCKS, N], BF16, name="x_sb")
-        nc.scalar.dma_start(x_sb[:], x.rearrange("(a p) n -> p a n", p=P))
+        nc.scalar.dma_start(x_sb[:], x.rearrange("(p a) n -> p a n", a=K_BLOCKS))
 
         ident_f32 = held.tile([P, P], F32, name="ident_f32")
         nc.vector.tensor_copy(ident_f32[:], ident[:])

@@ -65,5 +65,5 @@ def tile_scatter_matmul_kernel(tc, base, x, w, c, offs, out):
         for mb in range(M_BLOCKS):
             scaled = held.tile([P, S], F32, name=f"scaled{mb}")
             nc.vector.tensor_tensor(scaled[:], windows[mb][:], c_sb[:], mybir.AluOpType.mult)
-            store_queue = nc.sync if mb % 2 == 0 else nc.scalar
+            store_queue = nc.scalar if mb % 2 == 0 else nc.sync
             store_queue.dma_start(out[mb * P : (mb + 1) * P, :], scaled[:])

@@ -24,9 +24,11 @@ def tile_scatter_matmul_kernel(tc, base, x, w, c, offs, out):
         ident = held.tile([P, P], BF16, name="ident")
         make_identity(nc, ident[:])
 
+        zeros = held.tile([P, P], BF16, name="zeros")
+        nc.vector.memset(zeros[:], 0.0)
         warm_bank = banks.tile([P, P], F32, name="warm_bank")
         for i in range(WARM_UPS):
-            nc.tensor.matmul(warm_bank[:], ident[:], ident[:], start=True, stop=True)
+            nc.tensor.matmul(warm_bank[:], zeros[:], zeros[:], start=True, stop=True)
 
         c_col = held.tile([P, C_PLACES], F32, name="c_col")
         nc.scalar.dma_start(c_col[:], c.rearrange("o (p r) -> p (o r)", r=C_PLACES))

@@ -21,14 +21,17 @@ def tile_scatter_matmul_kernel(tc, base, x, w, c, offs, out):
         offsets = held.tile([P, N // 16], U16, name="offsets")
         nc.sync.dma_start(offsets[:], offs)
 
-        ident = held.tile([P, P], BF16, name="ident")
-        make_identity(nc, ident[:])
-
         zeros = held.tile([P, P], BF16, name="zeros")
         nc.vector.memset(zeros[:], 0.0)
         warm_bank = banks.tile([P, P], F32, name="warm_bank")
         for i in range(WARM_UPS):
             nc.tensor.matmul(warm_bank[:], zeros[:], zeros[:], start=True, stop=True)
+
+        ident_f32 = held.tile([P, P], F32, name="ident_f32")
+        nc.vector.memset(ident_f32[:], 0.0)
+        make_identity(nc, ident_f32[:], nomemset=True)
+        ident = held.tile([P, P], BF16, name="ident")
+        nc.vector.tensor_copy(ident[:], ident_f32[:])
 
         c_col = held.tile([P, C_PLACES], F32, name="c_col")
         nc.scalar.dma_start(c_col[:], c.rearrange("o (p r) -> p (o r)", r=C_PLACES))
@@ -40,8 +43,6 @@ def tile_scatter_matmul_kernel(tc, base, x, w, c, offs, out):
         x_sb = held.tile([P, K_BLOCKS, N], BF16, name="x_sb")
         nc.scalar.dma_start(x_sb[:], x.rearrange("(p a) n -> p a n", a=K_BLOCKS))
 
-        ident_f32 = held.tile([P, P], F32, name="ident_f32")
-        nc.vector.tensor_copy(ident_f32[:], ident[:])
         c_bank = banks.tile([P, C_PLACES, P], F32, name="c_bank")
         for r in range(C_PLACES):
             nc.tensor.transpose(c_bank[:, r, :], c_col[:, r : r + 1].to_broadcast([P, P]), ident_f32[:])

@@ -18,9 +18,6 @@ def tile_scatter_matmul_kernel(tc, base, x, w, c, offs, out):
         tc.tile_pool(name="held", bufs=1) as held,
         tc.psum_pool(name="banks", bufs=1) as banks,
     ):
-        offsets = held.tile([P, N // 16], U16, name="offsets")
-        nc.sync.dma_start(offsets[:], offs)
-
         zeros = held.tile([P, P], BF16, name="zeros")
         nc.vector.memset(zeros[:], 0.0)
         warm_bank = banks.tile([P, P], F32, name="warm_bank")
@@ -42,6 +39,8 @@ def tile_scatter_matmul_kernel(tc, base, x, w, c, offs, out):
         nc.sync.dma_start(w_sb[:], w.rearrange("(p a) m -> p a m", a=K_BLOCKS))
         x_sb = held.tile([P, K_BLOCKS, N], BF16, name="x_sb")
         nc.scalar.dma_start(x_sb[:], x.rearrange("(p a) n -> p a n", a=K_BLOCKS))
+        offsets = held.tile([P, N // 16], U16, name="offsets")
+        nc.sync.dma_start(offsets[:], offs)
 
         c_bank = banks.tile([P, C_PLACES, P], F32, name="c_bank")
         for r in range(C_PLACES):

@@ -6,7 +6,7 @@ S, K, M, N = 512, 256, 256, 256
 K_BLOCKS = K // P
 M_BLOCKS = M // P
 C_PLACES = S // P
-WARM_UPS = 8
+WARM_UPS = 12
 FLOPS = 2 * K * M * N
 
 BF16, F32, U16 = mybir.dt.bfloat16, mybir.dt.float32, mybir.dt.uint16

@@ -5,7 +5,9 @@ P = 128
 S, K, M, N = 512, 256, 256, 256
 K_BLOCKS = K // P
 M_BLOCKS = M // P
-C_PLACES = S // P
+SQUARE = 32
+GROUPS = P // SQUARE
+C_RUN = S // SQUARE
 WARM_UPS = 12
 FLOPS = 2 * K * M * N
 
@@ -24,14 +26,15 @@ def tile_scatter_matmul_kernel(tc, base, x, w, c, offs, out):
         for i in range(WARM_UPS):
             nc.tensor.matmul(warm_bank[:], zeros[:], zeros[:], start=True, stop=True)
 
-        ident_f32 = held.tile([P, P], F32, name="ident_f32")
-        nc.vector.memset(ident_f32[:], 0.0)
-        make_identity(nc, ident_f32[:], nomemset=True)
         ident = held.tile([P, P], BF16, name="ident")
-        nc.vector.tensor_copy(ident[:], ident_f32[:])
+        nc.vector.memset(ident[:], 0.0)
+        make_identity(nc, ident[:], nomemset=True)
 
-        c_col = held.tile([P, C_PLACES], F32, name="c_col")
-        nc.scalar.dma_start(c_col[:], c.rearrange("o (p r) -> p (o r)", r=C_PLACES))
+        c_piece = held.tile([P, C_RUN], F32, name="c_piece")
+        nc.scalar.dma_start(
+            c_piece[:],
+            c.rearrange("o (i u) -> o i u", u=C_RUN).to_broadcast([GROUPS, SQUARE, C_RUN]),
+        )
         base_sb = [held.tile([P, S], BF16, name=f"base_sb{mb}") for mb in range(M_BLOCKS)]
         nc.sync.dma_start(base_sb[0][:], base[0:P, :])
         nc.scalar.dma_start(base_sb[1][:], base[P : 2 * P, :])
@@ -42,12 +45,16 @@ def tile_scatter_matmul_kernel(tc, base, x, w, c, offs, out):
         offsets = held.tile([P, N // 16], U16, name="offsets")
         nc.sync.dma_start(offsets[:], offs)
 
-        c_bank = banks.tile([P, C_PLACES, P], F32, name="c_bank")
-        for r in range(C_PLACES):
-            nc.tensor.transpose(c_bank[:, r, :], c_col[:, r : r + 1].to_broadcast([P, P]), ident_f32[:])
+        c_rows = held.tile([P, S], F32, name="c_rows", align_bytes=64)
+        nc.vector.tensor_copy(
+            c_rows[:].rearrange("p (u j) -> p u j", j=SQUARE),
+            c_piece[:].unsqueeze(2).to_broadcast([P, C_RUN, SQUARE]),
+        )
+        c_turned = held.tile([P, S], F32, name="c_turned", align_bytes=64)
+        nc.vector.transpose(c_turned[:], c_rows[:])
         c_sb = held.tile([P, S], F32, name="c_sb")
         nc.vector.tensor_copy(
-            c_sb[:].rearrange("p (k r) -> p k r", r=C_PLACES), c_bank[:].rearrange("p r k -> p k r")
+            c_sb[:].rearrange("p (i u) -> p i u", u=C_RUN), c_turned[:].rearrange("p (u i) -> p i u", i=SQUARE)
         )
 
         windows = [banks.tile([P, S], F32, name=f"window{mb}") for mb in range(M_BLOCKS)]

@@ -6,8 +6,8 @@ S, K, M, N = 512, 256, 256, 256
 K_BLOCKS = K // P
 M_BLOCKS = M // P
 SQUARE = 32
-GROUPS = P // SQUARE
-C_RUN = S // SQUARE
+C_SQUARES = S // SQUARE
+C_COPIES = P // C_SQUARES
 WARM_UPS = 12
 FLOPS = 2 * K * M * N
 
@@ -30,10 +30,10 @@ def tile_scatter_matmul_kernel(tc, base, x, w, c, offs, out):
         nc.vector.memset(ident[:], 0.0)
         make_identity(nc, ident[:], nomemset=True)
 
-        c_piece = held.tile([P, C_RUN], F32, name="c_piece")
+        c_loaded = held.tile([P, SQUARE], F32, name="c_loaded", align_bytes=64)
         nc.scalar.dma_start(
-            c_piece[:],
-            c.rearrange("o (i u) -> o i u", u=C_RUN).to_broadcast([GROUPS, SQUARE, C_RUN]),
+            c_loaded[:],
+            c.rearrange("o (b i) -> o b i", i=SQUARE).to_broadcast([C_COPIES, C_SQUARES, SQUARE]),
         )
         base_sb = [held.tile([P, S], BF16, name=f"base_sb{mb}") for mb in range(M_BLOCKS)]
         nc.sync.dma_start(base_sb[0][:], base[0:P, :])
@@ -45,17 +45,15 @@ def tile_scatter_matmul_kernel(tc, base, x, w, c, offs, out):
         offsets = held.tile([P, N // 16], U16, name="offsets")
         nc.sync.dma_start(offsets[:], offs)
 
+        c_spaced = held.tile([P, SQUARE], F32, name="c_spaced", align_bytes=64)
+        nc.vector.transpose(c_spaced[:], c_loaded[:])
         c_rows = held.tile([P, S], F32, name="c_rows", align_bytes=64)
         nc.vector.tensor_copy(
-            c_rows[:].rearrange("p (u j) -> p u j", j=SQUARE),
-            c_piece[:].unsqueeze(2).to_broadcast([P, C_RUN, SQUARE]),
+            c_rows[:].rearrange("p (b j) -> p b j", j=SQUARE),
+            c_spaced[:, 0:C_SQUARES].unsqueeze(2).to_broadcast([P, C_SQUARES, SQUARE]),
         )
-        c_turned = held.tile([P, S], F32, name="c_turned", align_bytes=64)
-        nc.vector.transpose(c_turned[:], c_rows[:])
-        c_sb = held.tile([P, S], F32, name="c_sb")
-        nc.vector.tensor_copy(
-            c_sb[:].rearrange("p (i u) -> p i u", u=C_RUN), c_turned[:].rearrange("p (u i) -> p i u", i=SQUARE)
-        )
+        c_sb = held.tile([P, S], F32, name="c_sb", align_bytes=64)
+        nc.vector.transpose(c_sb[:], c_rows[:])
 
         windows = [banks.tile([P, S], F32, name=f"window{mb}") for mb in range(M_BLOCKS)]
         for mb in range(M_BLOCKS):

@@ -37,7 +37,7 @@ def tile_scatter_matmul_kernel(tc, base, x, w, c, offs, out):
         )
         base_sb = [held.tile([P, S], BF16, name=f"base_sb{mb}") for mb in range(M_BLOCKS)]
         nc.sync.dma_start(base_sb[0][:], base[0:P, :])
-        nc.scalar.dma_start(base_sb[1][:], base[P : 2 * P, :])
+        nc.sync.dma_start(base_sb[1][:], base[P : 2 * P, :])
         w_sb = held.tile([P, K_BLOCKS, M], BF16, name="w_sb")
         nc.sync.dma_start(w_sb[:], w.rearrange("(p a) m -> p a m", a=K_BLOCKS))
         x_sb = held.tile([P, K_BLOCKS, N], BF16, name="x_sb")

@@ -8,7 +8,7 @@ M_BLOCKS = M // P
 SQUARE = 32
 C_SQUARES = S // SQUARE
 C_COPIES = P // C_SQUARES
-WARM_UPS = 12
+WARM_UPS = 3
 FLOPS = 2 * K * M * N
 
 BF16, F32, U16 = mybir.dt.bfloat16, mybir.dt.float32, mybir.dt.uint16
@@ -22,9 +22,11 @@ def tile_scatter_matmul_kernel(tc, base, x, w, c, offs, out):
     ):
         zeros = held.tile([P, P], BF16, name="zeros")
         nc.vector.memset(zeros[:], 0.0)
-        warm_bank = banks.tile([P, P], F32, name="warm_bank")
+        warm_bank = banks.tile([P, S // P, P], F32, name="warm_bank")
         for i in range(WARM_UPS):
-            nc.tensor.matmul(warm_bank[:], zeros[:], zeros[:], start=True, stop=True)
+            nc.tensor.matmul(
+                warm_bank[:], zeros[:], zeros[:].unsqueeze(1).to_broadcast([P, S // P, P]), start=True, stop=True
+            )
 
         ident = held.tile([P, P], BF16, name="ident")
         nc.vector.memset(ident[:], 0.0)

@@ -40,13 +40,12 @@ def tile_scatter_matmul_kernel(tc, base, x, w, c, offs, out):
         base_sb = [held.tile([P, S], BF16, name=f"base_sb{mb}") for mb in range(M_BLOCKS)]
         nc.sync.dma_start(base_sb[0][:], base[0:P, :])
         nc.sync.dma_start(base_sb[1][:], base[P : 2 * P, :])
+        offsets = held.tile([P, N // 16], U16, name="offsets")
+        nc.sync.dma_start(offsets[:], offs)
         w_sb = held.tile([P, K_BLOCKS, M], BF16, name="w_sb")
         nc.sync.dma_start(w_sb[:], w.rearrange("(p a) m -> p a m", a=K_BLOCKS))
         x_sb = held.tile([P, K_BLOCKS, N], BF16, name="x_sb")
         nc.scalar.dma_start(x_sb[:], x.rearrange("(p a) n -> p a n", a=K_BLOCKS))
-        offsets = held.tile([P, N // 16], U16, name="offsets")
-        nc.sync.dma_start(offsets[:], offs)
-
         c_spaced = held.tile([P, SQUARE], F32, name="c_spaced", align_bytes=64)
         nc.vector.transpose(c_spaced[:], c_loaded[:])
         c_rows = held.tile([P, S], F32, name="c_rows", align_bytes=64)

@@ -8,6 +8,7 @@ M_BLOCKS = M // P
 SQUARE = 32
 C_SQUARES = S // SQUARE
 C_COPIES = P // C_SQUARES
+C_HALF = C_SQUARES // 2
 WARM_UPS = 3
 FLOPS = 2 * K * M * N
 
@@ -48,13 +49,15 @@ def tile_scatter_matmul_kernel(tc, base, x, w, c, offs, out):
         nc.scalar.dma_start(x_sb[:], x.rearrange("(p a) n -> p a n", a=K_BLOCKS))
         c_spaced = held.tile([P, SQUARE], F32, name="c_spaced", align_bytes=64)
         nc.vector.transpose(c_spaced[:], c_loaded[:])
-        c_rows = held.tile([P, S], F32, name="c_rows", align_bytes=64)
-        nc.vector.tensor_copy(
-            c_rows[:].rearrange("p (b j) -> p b j", j=SQUARE),
-            c_spaced[:, 0:C_SQUARES].unsqueeze(2).to_broadcast([P, C_SQUARES, SQUARE]),
-        )
         c_sb = held.tile([P, S], F32, name="c_sb", align_bytes=64)
-        nc.vector.transpose(c_sb[:], c_rows[:])
+        c_rows = [held.tile([P, S // 2], F32, name=f"c_rows{h}", align_bytes=64) for h in range(2)]
+        for h, engine in enumerate((nc.vector, nc.gpsimd)):
+            engine.tensor_copy(
+                c_rows[h][:].rearrange("p (b j) -> p b j", j=SQUARE),
+                c_spaced[:, h * C_HALF : (h + 1) * C_HALF].unsqueeze(2).to_broadcast([P, C_HALF, SQUARE]),
+            )
+        for h in range(2):
+            nc.vector.transpose(c_sb[:, h * (S // 2) : (h + 1) * (S // 2)], c_rows[h][:])
 
         windows = [banks.tile([P, S], F32, name=f"window{mb}") for mb in range(M_BLOCKS)]
         for mb in range(M_BLOCKS):

import concourse.mybir as mybir
from concourse.masks import make_identity

P = 128
S, K, M, N = 512, 256, 256, 256
K_BLOCKS = K // P
M_BLOCKS = M // P
SQUARE = 32
C_SQUARES = S // SQUARE
C_COPIES = P // C_SQUARES
C_HALF = C_SQUARES // 2
WARM_UPS = 3
FLOPS = 2 * K * M * N

BF16, F32, U16 = mybir.dt.bfloat16, mybir.dt.float32, mybir.dt.uint16


def tile_scatter_matmul_kernel(tc, base, x, w, c, offs, out):
    nc = tc.nc
    with (
        tc.tile_pool(name="held", bufs=1) as held,
        tc.psum_pool(name="banks", bufs=1) as banks,
    ):
        zeros = held.tile([P, P], BF16, name="zeros")
        nc.vector.memset(zeros[:], 0.0)
        warm_bank = banks.tile([P, S // P, P], F32, name="warm_bank")
        for i in range(WARM_UPS):
            nc.tensor.matmul(
                warm_bank[:], zeros[:], zeros[:].unsqueeze(1).to_broadcast([P, S // P, P]), start=True, stop=True
            )

        ident = held.tile([P, P], BF16, name="ident")
        nc.vector.memset(ident[:], 0.0)
        make_identity(nc, ident[:], nomemset=True)

        c_loaded = held.tile([P, SQUARE], F32, name="c_loaded", align_bytes=64)
        nc.scalar.dma_start(
            c_loaded[:],
            c.rearrange("o (b i) -> o b i", i=SQUARE).to_broadcast([C_COPIES, C_SQUARES, SQUARE]),
        )
        base_sb = [held.tile([P, S], BF16, name=f"base_sb{mb}") for mb in range(M_BLOCKS)]
        nc.sync.dma_start(base_sb[0][:], base[0:P, :])
        nc.sync.dma_start(base_sb[1][:], base[P : 2 * P, :])
        offsets = held.tile([P, N // 16], U16, name="offsets")
        nc.sync.dma_start(offsets[:], offs)
        w_sb = held.tile([P, K_BLOCKS, M], BF16, name="w_sb")
        nc.sync.dma_start(w_sb[:], w.rearrange("(p a) m -> p a m", a=K_BLOCKS))
        x_sb = held.tile([P, K_BLOCKS, N], BF16, name="x_sb")
        nc.scalar.dma_start(x_sb[:], x.rearrange("(p a) n -> p a n", a=K_BLOCKS))
        c_spaced = held.tile([P, SQUARE], F32, name="c_spaced", align_bytes=64)
        nc.vector.transpose(c_spaced[:], c_loaded[:])
        c_sb = held.tile([P, S], F32, name="c_sb", align_bytes=64)
        c_rows = [held.tile([P, S // 2], F32, name=f"c_rows{h}", align_bytes=64) for h in range(2)]
        for h, engine in enumerate((nc.vector, nc.gpsimd)):
            engine.tensor_copy(
                c_rows[h][:].rearrange("p (b j) -> p b j", j=SQUARE),
                c_spaced[:, h * C_HALF : (h + 1) * C_HALF].unsqueeze(2).to_broadcast([P, C_HALF, SQUARE]),
            )
        for h in range(2):
            nc.vector.transpose(c_sb[:, h * (S // 2) : (h + 1) * (S // 2)], c_rows[h][:])

        windows = [banks.tile([P, S], F32, name=f"window{mb}") for mb in range(M_BLOCKS)]
        for mb in range(M_BLOCKS):
            nc.tensor.matmul(windows[mb][:], ident[:], base_sb[mb][:], start=True, stop=False)

        for mb in range(M_BLOCKS):
            for kb in range(K_BLOCKS):
                nc.tensor.matmul(
                    windows[mb][:].indirect(offsets[:]),
                    w_sb[:, kb, mb * P : (mb + 1) * P],
                    x_sb[:, kb, :],
                    start=False,
                    stop=(kb == K_BLOCKS - 1),
                )

        for mb in range(M_BLOCKS):
            scaled = held.tile([P, S], F32, name=f"scaled{mb}")
            nc.vector.tensor_tensor(scaled[:], windows[mb][:], c_sb[:], mybir.AluOpType.mult)
            store_queue = nc.scalar if mb % 2 == 0 else nc.sync
            store_queue.dma_start(out[mb * P : (mb + 1) * P, :], scaled[:])
